import numpy as np
import ml_dtypes


def mxq(x, axis, fmt="e4m3"):
    dtype, down = {"e4m3": (ml_dtypes.float8_e4m3fn, 7), "e5m2": (ml_dtypes.float8_e5m2, 14)}[fmt]
    v = np.moveaxis(np.asarray(x, np.float32).astype(ml_dtypes.bfloat16).astype(np.float64), axis, -1)
    blocks = v.reshape(v.shape[:-1] + (-1, 32))
    amax = np.abs(blocks).max(-1, keepdims=True)
    byte = np.maximum(np.where(amax > 0, np.frexp(amax)[1] - 1 + 127, 0) - down, 1)
    scale = np.exp2(byte - 127.0)
    codes = (blocks / scale).astype(np.float32).astype(dtype).astype(np.float64)
    return np.moveaxis((codes * scale).reshape(v.shape), -1, axis)


WIDE = False


def mx_kscale(k):
    if not WIDE:
        return np.ones(k)
    levels = np.array([10, -10, 5, -5, 0])
    if k % 512:
        return np.exp2(np.random.permutation(np.resize(levels, k // 32))).repeat(32)
    a = np.empty((k // 512, 16))
    for p in range(k // 512):
        a[p, :8] = np.random.permutation(np.resize(levels, 8))
        for g in range(8):
            far = levels[np.abs(levels - a[p, g]) >= 10]
            a[p, g + 8] = far[np.random.randint(len(far))]
    return np.exp2(a.ravel()).repeat(32)


def f64(x):
    return np.asarray(x).astype(np.float64)


def striped(idx):
    return np.tile(np.asarray(idx).reshape(-1, 16).T, (8, 1)).astype(np.uint16)


def unstriped(offs):
    return offs[:16].T.reshape(-1).astype(np.int64)


E2M1 = np.array([0.0, 0.5, 1.0, 1.5, 2.0, 3.0, 4.0, 6.0, -0.0, -0.5, -1.0, -1.5, -2.0, -3.0, -4.0, -6.0])


def pack_weight(w, fmt):
    k, n = w.shape
    w = f64(np.asarray(w, np.float32).astype(ml_dtypes.bfloat16)).reshape(k // 32, 32, n)
    amax = np.abs(w).max(1)
    if fmt == "e4m3":
        byte = np.frexp(amax)[1] - 1 + 127 - 7
    else:
        mant, ex = np.frexp(amax / 6.0)
        byte = np.where(mant > 0.5, ex, ex - 1) + 127
    byte = np.clip(np.where(amax > 0, byte, 1), 1, 254)
    scaled = (w * np.exp2(127.0 - byte)[:, None, :]).reshape(k, n).astype(np.float32)
    by_word = np.ascontiguousarray(scaled.reshape(k // 512, 128, 4, n).transpose(0, 1, 3, 2))
    if fmt == "e4m3":
        words = by_word.astype(ml_dtypes.float8_e4m3fn).view(np.uint8)
    else:
        c = by_word.astype(ml_dtypes.float4_e2m1fn).view(np.uint8) & 0xF
        words = (c[..., 0::2] | (c[..., 1::2] << 4)).reshape(k // 512, 128, 2 * n)
    return np.ascontiguousarray(words), np.ascontiguousarray(byte.astype(np.uint8).reshape(k // 512, 16, n))


def unpack_weight(words, scales, fmt):
    g, _, n = scales.shape
    words = np.ascontiguousarray(words).reshape(g, 128, n, -1)
    if fmt == "e4m3":
        vals = words.view(ml_dtypes.float8_e4m3fn).astype(np.float64)
    else:
        nib = np.empty((g, 128, n, 4), np.uint8)
        nib[..., 0::2] = words & 0xF
        nib[..., 1::2] = words >> 4
        vals = E2M1[nib]
    vals = vals * np.repeat(np.exp2(scales.astype(np.float64) - 127.0), 8, axis=1)[..., None]
    return vals.transpose(0, 1, 3, 2).reshape(g * 512, n)


def softplus(v):
    return np.log(1.0 + np.exp(v))


def sigmoid(v):
    return 1.0 / (1.0 + np.exp(-v))


D, E, T, I, Q = 512, 512, 2048, 512, 128


def setup_inputs():
    n = np.random.standard_normal
    idx = np.random.permutation(T)[:I]
    fd = mx_kscale(D)
    fe = mx_kscale(E)
    fi = mx_kscale(I)
    ti = np.ones(T)
    ti[idx] = fi
    keysp = pack_weight(n((D, T)) / fd[:, None], "e2m1")
    valsp = pack_weight(n((E, T)) / fe[:, None], "e2m1")
    return {
        "query": (n((D, Q)) * 1.0 / np.sqrt(D) * fd[:, None]).astype(np.float32),
        "keys_words": keysp[0],
        "keys_scales": keysp[1],
        "th": (np.random.uniform(-0.5, 0.5, (Q, 1))).astype(np.float32),
        "reserve": (np.random.uniform(20.0, 100.0, (Q, 1))).astype(np.float32),
        "gout": (n((E, Q)) * 1 / np.sqrt(E) * fe[:, None]).astype(np.float32),
        "vals_words": valsp[0],
        "vals_scales": valsp[1],
        "size": (np.random.uniform(0.5, 2.0, (1, I))).astype(np.float32),
        "dquery": (n((D, Q)) * 1.0 / np.sqrt(D) * fd[:, None]).astype(np.float32),
        "fs": (np.random.uniform(128.0, 512.0, (1, I)) * fi).astype(np.float32),
        "keyrows": (n((D, T)) / ti).astype(np.float32),
        "res": (n((Q, D)) * 4.0).astype(np.float32),
        "offs": striped(idx),
    }


def reference(query, keys_words, keys_scales, th, reserve, gout, vals_words, vals_scales, size, dquery, fs, keyrows, res, offs):
    idx = unstriped(offs)
    keysu = unpack_weight(keys_words, keys_scales, "e2m1")
    valsu = unpack_weight(vals_words, vals_scales, "e2m1")
    queryq = mxq(f64(query), 0, "e4m3")
    keysidxg = keysu[:, idx]
    a = queryq.T @ keysidxg
    dqueryq = mxq(f64(dquery), 0, "e4m3")
    ta = dqueryq.T @ keysidxg
    p = softplus(a - f64(th))
    z = np.sum(p, axis=1, keepdims=True) + f64(reserve)
    goutq = mxq(f64(gout), 0, "e4m3")
    valsidxg = valsu[:, idx]
    c0 = goutq.T @ valsidxg
    dz = np.sum(c0 * p * f64(size) / np.square(z) * (-1.0), axis=1, keepdims=True)
    dp = c0 / z * f64(size) + dz
    tp = ta * sigmoid(a - f64(th))
    tz = np.sum(tp, axis=1, keepdims=True)
    tdz = np.sum((tp * f64(size) * c0 - tz * z * 2.0 * c0 * p * f64(size) / np.square(z)) / np.square(z) * (-1.0), axis=1, keepdims=True)
    tdp = tz * c0 / np.square(z) * (-1.0) * f64(size) + tdz
    tda = tdp * sigmoid(a - f64(th)) + ta * sigmoid(a - f64(th)) * (1.0 - sigmoid(a - f64(th))) * dp
    gs = tda * f64(fs)
    gt1 = gs.T
    kt = f64(keyrows)[:, idx].T
    gt1q = mxq(gt1, 0, "e4m3")
    ktq = mxq(kt, 0, "e4m3")
    gq = gt1q.T @ ktq
    y = gq + f64(res)
    return y

@@ -1,0 +1,275 @@
+from contextlib import ExitStack
+
+import concourse.mybir as mybir
+from concourse.masks import make_identity
+
+F32 = mybir.dt.float32
+BF16 = mybir.dt.bfloat16
+I32 = mybir.dt.int32
+U32 = mybir.dt.uint32
+U16 = mybir.dt.uint16
+U8 = mybir.dt.uint8
+FP8X4 = mybir.dt.float8_e4m3fn_x4
+FP4X4 = mybir.dt.float4_e2m1fn_x4
+ALU = mybir.AluOpType
+ACT = mybir.ActivationFunctionType
+
+P = 128
+PACK = 4
+D, E, T, I, Q = 512, 512, 2048, 512, 128
+FLOPS = 2 * Q * I * (2 * D + E + D)
+
+
+def tile_attend_hvsoftthreshold_q_kernel(
+    tc, query, keys_words, keys_scales, th, reserve, gout, vals_words, vals_scales,
+    size, dquery, fs, keyrows, res, offs, out,
+):
+    nc = tc.nc
+    with ExitStack() as ctx:
+        sb = ctx.enter_context(tc.tile_pool(name="sb", bufs=1))
+        ps = ctx.enter_context(tc.psum_pool(name="ps", bufs=1))
+
+        def tile(name, shape, dtype, tag=None):
+            return sb.tile(shape, dtype, name=name, tag=tag or name, align_bytes=64)
+
+        def column(name, tag=None):
+            return tile(name, [P, 1], F32, tag)
+
+        def dealt(bank):
+            return bank[:].rearrange("q (p t) -> q t p", t=PACK)
+
+        key_scales = tile("key_scales", [P, T], U8)
+        val_scales = tile("val_scales", [P, T], U8)
+        nc.vector.memset(key_scales[:].bitcast(I32), 0)
+        nc.gpsimd.memset(val_scales[:].bitcast(I32), 0)
+        warm_in = column("warm_in")
+        warm_out = column("warm_out")
+        nc.vector.memset(warm_in[:], 0.0)
+        nc.scalar.activation(out=warm_out[:], in_=warm_in[:], func=ACT.Sigmoid)
+
+        offsets = sb.tile([P, I // 16], U16, name="offsets")
+        nc.sync.dma_start(offsets[:], offs)
+
+        def load_words(name, words):
+            pool_words = tile(name, [P, T], U16)
+            nc.sync.dma_start(pool_words[:].bitcast(I32), words[0].bitcast(I32))
+            return pool_words
+
+        def load_scales(plane, scales):
+            for quad in range(4):
+                nc.sync.dma_start(
+                    plane[32 * quad : 32 * quad + 4, :].bitcast(I32),
+                    scales[0, 4 * quad : 4 * quad + 4, :].bitcast(I32),
+                )
+
+        def load_rows(name, rows):
+            raw = tile(name, [P, PACK, Q], F32)
+            nc.sync.dma_start(raw[:], rows.rearrange("(p t) q -> p t q", t=PACK))
+            return raw
+
+        load_scales(key_scales, keys_scales)
+        key_words = load_words("key_words", keys_words)
+        query_raw = load_rows("query_raw", query)
+        dquery_raw = load_rows("dquery_raw", dquery)
+        gout_raw = load_rows("gout_raw", gout)
+        load_scales(val_scales, vals_scales)
+        val_words = load_words("val_words", vals_words)
+        size_col = tile("size_col", [P, I // P], F32)
+        with nc.allow_non_contiguous_dma(reason="one size a partition and slot tile"):
+            nc.sync.dma_start(size_col[:], size.rearrange("o (j m) -> m (o j)", m=P))
+        th_col = column("th_col")
+        nc.gpsimd.dma_start(th_col[:], th)
+        reserve_col = column("reserve_col")
+        nc.gpsimd.dma_start(reserve_col[:], reserve)
+        fs_col = sb.tile([P, PACK], F32, name="fs_col")
+        nc.gpsimd.dma_start(fs_col[:], fs.rearrange("o (p t) -> p (o t)", t=PACK))
+        key_rows = []
+        for c in range(D // P):
+            rows = tile("key_rows%d" % c, [P, T], F32)
+            nc.sync.dma_start(rows[:], keyrows[c * P : (c + 1) * P, :])
+            key_rows.append(rows)
+        res_sb = tile("res_sb", [P, D], F32)
+        nc.sync.dma_start(res_sb[:], res)
+
+        ident = tile("ident", [P, P], F32)
+        make_identity(nc, ident[:])
+        neg_th = column("neg_th")
+        nc.gpsimd.tensor_scalar(neg_th[:], th_col[:], -1.0, 0.0, ALU.mult, ALU.add)
+
+        def gather(name, window, dtype, tag=None):
+            picked = tile(name, [P, I], dtype, tag)
+            nc.vector.tensor_copy(picked[:], window[:].indirect(offsets[:]))
+            return picked
+
+        def quantize(name, grouped, columns):
+            codes = tile(name + "_codes", [P, columns], U32)
+            scales = tile(name + "_scales", [P, columns], U8)
+            nc.vector.quantize_mx(out=codes[:].bitcast(FP8X4), scales=scales[:], in_=grouped)
+            return codes, scales
+
+        key_scales_g = gather("key_scales_g", key_scales, U8)
+        key_words_g = gather("key_words_g", key_words, U16)
+        q_grouped = tile("q_grouped", [P, Q, PACK], BF16)
+        nc.scalar.copy(q_grouped[:], query_raw[:].rearrange("p t q -> p q t"))
+        q_codes, q_scales = quantize("q", q_grouped[:].rearrange("p q t -> p (q t)"), Q)
+
+        def key_scores(name, tag, codes, scales):
+            bank = ps.tile([P, I], F32, name=name, tag=tag)
+            nc.tensor.matmul_mx(
+                out=bank[:],
+                lhsT=codes.bitcast(FP8X4),
+                lhsT_scale=scales,
+                rhs=key_words_g[:].bitcast(FP4X4),
+                rhs_scale=key_scales_g[:],
+                start=True,
+                stop=True,
+            )
+            return bank
+
+        a_ps = key_scores("a_ps", "bank_a", q_codes[:], q_scales[:])
+        val_scales_g = gather("val_scales_g", val_scales, U8, "q_grouped")
+        dg_grouped = tile("dg_grouped", [P, 2, Q, PACK], BF16)
+        nc.scalar.copy(dg_grouped[:, 0], dquery_raw[:].rearrange("p t q -> p q t"))
+        nc.scalar.copy(dg_grouped[:, 1], gout_raw[:].rearrange("p t q -> p q t"))
+        dg_codes, dg_scales = quantize(
+            "dg", dg_grouped[:].rearrange("p s q t -> p (s q t)"), 2 * Q
+        )
+        ta_ps = key_scores("ta_ps", "bank_ta", dg_codes[:, 0:Q], dg_scales[:, 0:Q])
+        val_words_g = gather("val_words_g", val_words, U16, "dg_grouped")
+
+        sig = tile("sig", [P, PACK, P], F32)
+        nc.scalar.activation(out=sig[:], in_=dealt(a_ps), func=ACT.Sigmoid, bias=neg_th[:])
+        mag = tile("mag", [P, PACK, P], F32)
+        nc.scalar.activation(out=mag[:], in_=dealt(a_ps), func=ACT.Abs, bias=neg_th[:])
+        sig_mag = tile("sig_mag", [P, PACK, P], F32)
+        nc.scalar.activation(out=sig_mag[:], in_=mag[:], func=ACT.Sigmoid)
+        relu = tile("relu", [P, PACK, P], F32)
+        relu_sum = column("relu_sum")
+        nc.scalar.activation(
+            out=relu[:], in_=dealt(a_ps), func=ACT.Relu, bias=neg_th[:], accum_out=relu_sum[:]
+        )
+
+        c0t_ps = ps.tile([P, I // P, Q], F32, name="c0t_ps", tag="bank_c0")
+        for j in range(I // P):
+            nc.tensor.matmul_mx(
+                out=c0t_ps[:, j, :],
+                lhsT=val_words_g[:, j * P : (j + 1) * P].bitcast(FP4X4),
+                lhsT_scale=val_scales_g[:, j * P : (j + 1) * P],
+                rhs=dg_codes[:, Q : 2 * Q].bitcast(FP8X4),
+                rhs_scale=dg_scales[:, Q : 2 * Q],
+                start=True,
+                stop=True,
+            )
+        cst = tile("cst", [P, I // P, Q], F32)
+        for j in range(I // P):
+            nc.scalar.activation(
+                out=cst[:, j, :], in_=c0t_ps[:, j, :], func=ACT.Copy, scale=size_col[:, j : j + 1]
+            )
+        cs_v = ps.tile([P, I], F32, name="cs_v")
+        cs_s = ps.tile([P, I], F32, name="cs_s", tag="cs_s")
+        for bank in (cs_v, cs_s):
+            for j in range(I // P):
+                nc.tensor.transpose(bank[:, j * P : (j + 1) * P], cst[:, j, :], ident[:])
+
+        log_sig = tile("log_sig", [P, PACK, P], F32, "size_col")
+        log_sum = column("log_sum")
+        nc.scalar.activation(out=log_sig[:], in_=sig_mag[:], func=ACT.Ln, accum_out=log_sum[:])
+
+        tp = tile("tp", [P, PACK, P], F32)
+        tz = column("tz")
+        nc.vector.scalar_tensor_tensor(
+            tp[:], dealt(ta_ps), 1.0, sig[:], ALU.mult, ALU.mult, accum_out=tz[:]
+        )
+        neg_u = tile("neg_u", [P, PACK, P], F32)
+        nc.vector.scalar_tensor_tensor(neg_u[:], sig[:], 1.0, tp[:], ALU.subtract, ALU.mult)
+
+        kt_words = tile("kt_words", [P, D // P, P, PACK], BF16)
+
+        def turn_key_rows(c, tag=None):
+            picked = gather("kt_picked%d" % c, key_rows[c], BF16, tag)
+            pairs = picked[:].bitcast(F32)
+            turned = ps.tile([P, 2, P], F32, name="turned%d" % c, tag="bank_kt%d" % (c % 2))
+            for u in range(2):
+                nc.tensor.transpose(turned[:, u, :], pairs[:, u : I // 2 : 2], ident[:])
+            nc.scalar.copy(kt_words[:, c].bitcast(F32), turned[:].rearrange("p u d -> p d u"))
+
+        turn_key_rows(0)
+
+        def weighted_sum(name, other, tag=None):
+            product = tile(name + "_product", [P, PACK, P], F32, tag)
+            total = column(name)
+            nc.vector.scalar_tensor_tensor(
+                product[:], dealt(cs_v), 1.0, other[:], ALU.mult, ALU.mult, accum_out=total[:]
+            )
+            return total
+
+        cs_tp = weighted_sum("cs_tp", tp, "key_rows0")
+        cs_relu = weighted_sum("cs_relu", relu)
+        turn_key_rows(1, "relu")
+        z_part = column("z_part")
+        nc.gpsimd.tensor_tensor(z_part[:], relu_sum[:], reserve_col[:], ALU.add)
+        neg_z = column("neg_z", "key_rows1")
+        nc.vector.tensor_tensor(neg_z[:], log_sum[:], z_part[:], ALU.subtract)
+        neg_r = column("neg_r")
+        nc.vector.reciprocal(neg_r[:], neg_z[:])
+        cs_log = weighted_sum("cs_log", log_sig)
+        neg_r2 = column("neg_r2")
+        nc.gpsimd.tensor_scalar(neg_r2[:], neg_r[:], neg_r[:], -1.0, ALU.mult, ALU.mult)
+        beta = column("beta")
+        nc.gpsimd.tensor_tensor(beta[:], tz[:], neg_r2[:], ALU.mult)
+        b_term = column("b_term")
+        nc.gpsimd.tensor_tensor(b_term[:], cs_tp[:], neg_r2[:], ALU.mult)
+        dz_factor = column("dz_factor")
+        nc.gpsimd.tensor_scalar(dz_factor[:], tz[:], neg_r[:], 2.0, ALU.mult, ALU.mult)
+        neg_k = tile("neg_k", [P, PACK, P], F32)
+        nc.scalar.activation(out=neg_k[:], in_=dealt(cs_s), func=ACT.Copy, scale=neg_r[:])
+        dz = column("dz")
+        nc.vector.tensor_scalar(dz[:], cs_relu[:], cs_log[:], neg_r2[:], ALU.subtract, ALU.mult)
+        tdz = column("tdz")
+        nc.vector.tensor_scalar(tdz[:], dz[:], dz_factor[:], b_term[:], ALU.mult, ALU.add)
+        tdp = tile("tdp", [P, PACK, P], F32)
+        nc.scalar.activation(
+            out=tdp[:], in_=dealt(cs_s), func=ACT.Identity, scale=beta[:], bias=tdz[:]
+        )
+        turn_key_rows(2, "b_term")
+        curve = tile("curve", [P, PACK, P], F32, "key_rows2")
+        nc.vector.scalar_tensor_tensor(curve[:], neg_k[:], dz[:], neg_u[:], ALU.subtract, ALU.mult)
+        slope = tile("slope", [P, PACK, P], F32)
+        nc.vector.tensor_tensor(slope[:], tdp[:], sig[:], ALU.mult)
+
+        tda_t = ps.tile([P, PACK, Q], F32, name="tda_t", tag="bank_a")
+        for n, part in enumerate((curve, slope)):
+            for t in range(PACK):
+                nc.tensor.matmul(
+                    tda_t[:, t, :], lhsT=part[:, t, :], rhs=ident[:], is_transpose=True,
+                    start=(n == 0 and t == 0), stop=(n == 1 and t == PACK - 1),
+                )
+        turn_key_rows(3, "tdp")
+        gs_words = tile("gs_words", [P, Q, PACK], BF16, "key_rows3")
+        nc.vector.tensor_tensor(
+            gs_words[:],
+            tda_t[:].rearrange("p t q -> p q t"),
+            fs_col[:].unsqueeze(1).to_broadcast([P, Q, PACK]),
+            ALU.mult,
+        )
+        gs_codes, gs_scales = quantize("gs", gs_words[:].rearrange("p q t -> p (q t)"), Q)
+
+        for n, (first, last, bank) in enumerate(((0, 2, "bank_ta"), (2, 3, "bank_c0"), (3, 4, "cs_s"))):
+            width = (last - first) * P
+            cols = slice(first * P, last * P)
+            codes, scales = quantize(
+                "kt%d" % n, kt_words[:, first:last].rearrange("p c d t -> p (c d t)"), width
+            )
+            gq = ps.tile([P, width], F32, name="gq%d" % n, tag=bank)
+            nc.tensor.matmul_mx(
+                out=gq[:],
+                lhsT=gs_codes[:].bitcast(FP8X4),
+                lhsT_scale=gs_scales[:],
+                rhs=codes[:].bitcast(FP8X4),
+                rhs_scale=scales[:],
+                start=True,
+                stop=True,
+            )
+            result = tile("result%d" % n, [P, width], F32)
+            nc.vector.tensor_tensor(result[:], gq[:], res_sb[:, cols], ALU.add)
+            nc.sync.dma_start(out[:, cols], result[:])

@@ -41,7 +41,7 @@ def tile_attend_hvsoftthreshold_q_kernel(
         key_scales = tile("key_scales", [P, T], U8)
         val_scales = tile("val_scales", [P, T], U8)
         nc.vector.memset(key_scales[:].bitcast(I32), 0)
-        nc.gpsimd.memset(val_scales[:].bitcast(I32), 0)
+        nc.vector.memset(val_scales[:].bitcast(I32), 0)
         warm_in = column("warm_in")
         warm_out = column("warm_out")
         nc.vector.memset(warm_in[:], 0.0)
@@ -74,35 +74,40 @@ def tile_attend_hvsoftthreshold_q_kernel(
         gout_raw = load_rows("gout_raw", gout)
         load_scales(val_scales, vals_scales)
         val_words = load_words("val_words", vals_words)
+        th_col = column("th_col")
+        nc.sync.dma_start(th_col[:], th)
         size_col = tile("size_col", [P, I // P], F32)
         with nc.allow_non_contiguous_dma(reason="one size a partition and slot tile"):
             nc.sync.dma_start(size_col[:], size.rearrange("o (j m) -> m (o j)", m=P))
-        th_col = column("th_col")
-        nc.gpsimd.dma_start(th_col[:], th)
-        reserve_col = column("reserve_col")
-        nc.gpsimd.dma_start(reserve_col[:], reserve)
-        fs_col = sb.tile([P, PACK], F32, name="fs_col")
-        nc.gpsimd.dma_start(fs_col[:], fs.rearrange("o (p t) -> p (o t)", t=PACK))
         key_rows = []
-        for c in range(D // P):
+
+        def load_key_rows(c):
             rows = tile("key_rows%d" % c, [P, T], F32)
             nc.sync.dma_start(rows[:], keyrows[c * P : (c + 1) * P, :])
             key_rows.append(rows)
+
+        load_key_rows(0)
+        reserve_col = column("reserve_col")
+        nc.sync.dma_start(reserve_col[:], reserve)
+        fs_col = tile("fs_col", [P, PACK], F32)
+        nc.sync.dma_start(fs_col[:], fs.rearrange("o (p t) -> p (o t)", t=PACK))
+        for c in range(1, D // P):
+            load_key_rows(c)
         res_sb = tile("res_sb", [P, D], F32)
         nc.sync.dma_start(res_sb[:], res)
 
         ident = tile("ident", [P, P], F32)
         make_identity(nc, ident[:])
         neg_th = column("neg_th")
-        nc.gpsimd.tensor_scalar(neg_th[:], th_col[:], -1.0, 0.0, ALU.mult, ALU.add)
+        nc.scalar.activation(out=neg_th[:], in_=th_col[:], func=ACT.Copy, scale=-1.0)
 
         def gather(name, window, dtype, tag=None):
             picked = tile(name, [P, I], dtype, tag)
             nc.vector.tensor_copy(picked[:], window[:].indirect(offsets[:]))
             return picked
 
-        def quantize(name, grouped, columns):
-            codes = tile(name + "_codes", [P, columns], U32)
+        def quantize(name, grouped, columns, tag=None):
+            codes = tile(name + "_codes", [P, columns], U32, tag)
             scales = tile(name + "_scales", [P, columns], U8)
             nc.vector.quantize_mx(out=codes[:].bitcast(FP8X4), scales=scales[:], in_=grouped)
             return codes, scales
@@ -175,15 +180,14 @@ def tile_attend_hvsoftthreshold_q_kernel(
         log_sum = column("log_sum")
         nc.scalar.activation(out=log_sig[:], in_=sig_mag[:], func=ACT.Ln, accum_out=log_sum[:])
 
+        sums = tile("sums", [P, 3], F32)
+        neg_cs_relu, tz, cs_tp = (sums[:, n : n + 1] for n in range(3))
         tp = tile("tp", [P, PACK, P], F32)
-        tz = column("tz")
         nc.vector.scalar_tensor_tensor(
-            tp[:], dealt(ta_ps), 1.0, sig[:], ALU.mult, ALU.mult, accum_out=tz[:]
+            tp[:], dealt(ta_ps), 1.0, sig[:], ALU.mult, ALU.mult, accum_out=tz
         )
-        neg_u = tile("neg_u", [P, PACK, P], F32)
-        nc.vector.scalar_tensor_tensor(neg_u[:], sig[:], 1.0, tp[:], ALU.subtract, ALU.mult)
-
-        kt_words = tile("kt_words", [P, D // P, P, PACK], BF16)
+        neg_w = tile("neg_w", [P, PACK, P], F32)
+        nc.vector.scalar_tensor_tensor(neg_w[:], sig[:], 1.0, dealt(ta_ps), ALU.subtract, ALU.mult)
 
         def turn_key_rows(c, tag=None):
             picked = gather("kt_picked%d" % c, key_rows[c], BF16, tag)
@@ -191,75 +195,90 @@ def tile_attend_hvsoftthreshold_q_kernel(
             turned = ps.tile([P, 2, P], F32, name="turned%d" % c, tag="bank_kt%d" % (c % 2))
             for u in range(2):
                 nc.tensor.transpose(turned[:, u, :], pairs[:, u : I // 2 : 2], ident[:])
-            nc.scalar.copy(kt_words[:, c].bitcast(F32), turned[:].rearrange("p u d -> p d u"))
+            return turned
 
-        turn_key_rows(0)
+        def weave(words, turned):
+            nc.scalar.copy(words.bitcast(F32), turned[:].rearrange("p u d -> p d u"))
 
-        def weighted_sum(name, other, tag=None):
+        def quantize_kt(name, words, chunks, tag=None):
+            return quantize(name, words[:].rearrange("p c d t -> p (c d t)"), chunks * P, tag)
+
+        def weighted_sum(name, sign, other, total, tag=None):
             product = tile(name + "_product", [P, PACK, P], F32, tag)
-            total = column(name)
             nc.vector.scalar_tensor_tensor(
-                product[:], dealt(cs_v), 1.0, other[:], ALU.mult, ALU.mult, accum_out=total[:]
+                product[:], dealt(cs_v), sign, other[:], ALU.mult, ALU.mult, accum_out=total
             )
-            return total
 
-        cs_tp = weighted_sum("cs_tp", tp, "key_rows0")
-        cs_relu = weighted_sum("cs_relu", relu)
-        turn_key_rows(1, "relu")
-        z_part = column("z_part")
-        nc.gpsimd.tensor_tensor(z_part[:], relu_sum[:], reserve_col[:], ALU.add)
-        neg_z = column("neg_z", "key_rows1")
-        nc.vector.tensor_tensor(neg_z[:], log_sum[:], z_part[:], ALU.subtract)
-        neg_r = column("neg_r")
-        nc.vector.reciprocal(neg_r[:], neg_z[:])
-        cs_log = weighted_sum("cs_log", log_sig)
-        neg_r2 = column("neg_r2")
-        nc.gpsimd.tensor_scalar(neg_r2[:], neg_r[:], neg_r[:], -1.0, ALU.mult, ALU.mult)
-        beta = column("beta")
-        nc.gpsimd.tensor_tensor(beta[:], tz[:], neg_r2[:], ALU.mult)
-        b_term = column("b_term")
-        nc.gpsimd.tensor_tensor(b_term[:], cs_tp[:], neg_r2[:], ALU.mult)
-        dz_factor = column("dz_factor")
-        nc.gpsimd.tensor_scalar(dz_factor[:], tz[:], neg_r[:], 2.0, ALU.mult, ALU.mult)
-        neg_k = tile("neg_k", [P, PACK, P], F32)
-        nc.scalar.activation(out=neg_k[:], in_=dealt(cs_s), func=ACT.Copy, scale=neg_r[:])
-        dz = column("dz")
-        nc.vector.tensor_scalar(dz[:], cs_relu[:], cs_log[:], neg_r2[:], ALU.subtract, ALU.mult)
-        tdz = column("tdz")
-        nc.vector.tensor_scalar(tdz[:], dz[:], dz_factor[:], b_term[:], ALU.mult, ALU.add)
-        tdp = tile("tdp", [P, PACK, P], F32)
-        nc.scalar.activation(
-            out=tdp[:], in_=dealt(cs_s), func=ACT.Identity, scale=beta[:], bias=tdz[:]
-        )
-        turn_key_rows(2, "b_term")
+        def affine(name, x, scale, bias=None, shape=(P, 1)):
+            y = tile(name, list(shape), F32)
+            if bias is None:
+                nc.scalar.activation(out=y[:], in_=x, func=ACT.Copy, scale=scale)
+            else:
+                nc.scalar.activation(out=y[:], in_=x, func=ACT.Identity, scale=scale, bias=bias)
+            return y
+
+        z_part = affine("z_part", relu_sum[:], 1.0, reserve_col[:])
+        two_tz = affine("two_tz", tz, 2.0)
+        kt_first = tile("kt_first", [P, 1, P, PACK], BF16)
+        weave(kt_first[:, 0], turn_key_rows(0))
+        weighted_sum("cs_tp", 1.0, tp, cs_tp, "key_rows0")
+        weighted_sum("cs_relu", -1.0, relu, neg_cs_relu)
+        turned1 = turn_key_rows(1, "relu")
+        z = affine("z", log_sum[:], -1.0, z_part[:])
+
+        sig_t = ps.tile([P, PACK, Q], F32, name="sig_t")
+        for t in range(PACK):
+            nc.tensor.transpose(sig_t[:, t, :], sig[:, t, :], ident[:])
+        neg_fs = affine("neg_fs", fs_col[:], -1.0, shape=(P, PACK))
+        factor_planes = tile("factor_planes", [P, PACK, Q], F32)
+        for t in range(PACK):
+            nc.scalar.activation(
+                out=factor_planes[:, t, :], in_=sig_t[:, t, :], func=ACT.Copy,
+                scale=neg_fs[:, t : t + 1],
+            )
+
+        factor = tile("factor", [P, Q, PACK], F32)
+        nc.scalar.copy(factor[:], factor_planes[:].rearrange("p t q -> p q t"))
+        r = column("r", "key_rows1")
+        nc.vector.reciprocal(r[:], z[:])
+        cs_log = column("cs_log")
+        weighted_sum("cs_log", 1.0, log_sig, cs_log[:])
+        turned2 = turn_key_rows(2, "size_col")
+        r2 = column("r2")
+        nc.scalar.activation(out=r2[:], in_=r[:], func=ACT.Square)
+        scaled = affine("scaled", sums[:], r2[:], shape=(P, 3))
+        dz_factor = affine("dz_factor", two_tz[:], r[:])
+        dz = affine("dz", cs_log[:], r2[:], scaled[:, 0:1])
+        neg_tdz = affine("neg_tdz", dz[:], dz_factor[:], scaled[:, 2:3])
+        k = affine("k", dealt(cs_s), r[:], shape=(P, PACK, P))
+        neg_tdp = affine("neg_tdp", dealt(cs_s), scaled[:, 1:2], neg_tdz[:], shape=(P, PACK, P))
         curve = tile("curve", [P, PACK, P], F32, "key_rows2")
-        nc.vector.scalar_tensor_tensor(curve[:], neg_k[:], dz[:], neg_u[:], ALU.subtract, ALU.mult)
-        slope = tile("slope", [P, PACK, P], F32)
-        nc.vector.tensor_tensor(slope[:], tdp[:], sig[:], ALU.mult)
+        nc.vector.scalar_tensor_tensor(curve[:], k[:], dz[:], neg_w[:], ALU.add, ALU.mult)
+        kt_mid = tile("kt_mid", [P, 2, P, PACK], BF16, "neg_tdz")
+        weave(kt_mid[:, 0], turned1)
+        weave(kt_mid[:, 1], turned2)
 
         tda_t = ps.tile([P, PACK, Q], F32, name="tda_t", tag="bank_a")
-        for n, part in enumerate((curve, slope)):
+        for n, part in enumerate((neg_tdp, curve)):
             for t in range(PACK):
                 nc.tensor.matmul(
                     tda_t[:, t, :], lhsT=part[:, t, :], rhs=ident[:], is_transpose=True,
                     start=(n == 0 and t == 0), stop=(n == 1 and t == PACK - 1),
                 )
-        turn_key_rows(3, "tdp")
-        gs_words = tile("gs_words", [P, Q, PACK], BF16, "key_rows3")
+        kt_last = tile("kt_last", [P, 1, P, PACK], BF16)
+        weave(kt_last[:, 0], turn_key_rows(3, "neg_w"))
+        kt_quant = [quantize_kt("kt0", kt_first, 1), quantize_kt("kt1", kt_mid, 2, "key_rows3")]
+        gs_words = tile("gs_words", [P, Q, PACK], BF16, "neg_tdz")
         nc.vector.tensor_tensor(
-            gs_words[:],
-            tda_t[:].rearrange("p t q -> p q t"),
-            fs_col[:].unsqueeze(1).to_broadcast([P, Q, PACK]),
-            ALU.mult,
+            gs_words[:], tda_t[:].rearrange("p t q -> p q t"), factor[:], ALU.mult
         )
         gs_codes, gs_scales = quantize("gs", gs_words[:].rearrange("p q t -> p (q t)"), Q)
+        kt_quant.append(quantize_kt("kt2", kt_last, 1))
 
-        for n, (first, last, bank) in enumerate(((0, 2, "bank_ta"), (2, 3, "bank_c0"), (3, 4, "cs_s"))):
+        for n, (first, last, bank) in enumerate(((0, 1, "bank_ta"), (1, 3, "bank_c0"), (3, 4, "cs_s"))):
             width = (last - first) * P
             cols = slice(first * P, last * P)
-            codes, scales = quantize(
-                "kt%d" % n, kt_words[:, first:last].rearrange("p c d t -> p (c d t)"), width
-            )
+            codes, scales = kt_quant[n]
             gq = ps.tile([P, width], F32, name="gq%d" % n, tag=bank)
             nc.tensor.matmul_mx(
                 out=gq[:],

@@ -112,8 +112,16 @@ def tile_attend_hvsoftthreshold_q_kernel(
             nc.vector.quantize_mx(out=codes[:].bitcast(FP8X4), scales=scales[:], in_=grouped)
             return codes, scales
 
-        key_scales_g = gather("key_scales_g", key_scales, U8)
+        def affine(name, x, scale, bias=None, shape=(P, 1)):
+            y = tile(name, list(shape), F32)
+            if bias is None:
+                nc.scalar.activation(out=y[:], in_=x, func=ACT.Copy, scale=scale)
+            else:
+                nc.scalar.activation(out=y[:], in_=x, func=ACT.Identity, scale=scale, bias=bias)
+            return y
+
         key_words_g = gather("key_words_g", key_words, U16)
+        key_scales_g = gather("key_scales_g", key_scales, U8)
         q_grouped = tile("q_grouped", [P, Q, PACK], BF16)
         nc.scalar.copy(q_grouped[:], query_raw[:].rearrange("p t q -> p q t"))
         q_codes, q_scales = quantize("q", q_grouped[:].rearrange("p q t -> p (q t)"), Q)
@@ -132,7 +140,6 @@ def tile_attend_hvsoftthreshold_q_kernel(
             return bank
 
         a_ps = key_scores("a_ps", "bank_a", q_codes[:], q_scales[:])
-        val_scales_g = gather("val_scales_g", val_scales, U8, "q_grouped")
         dg_grouped = tile("dg_grouped", [P, 2, Q, PACK], BF16)
         nc.scalar.copy(dg_grouped[:, 0], dquery_raw[:].rearrange("p t q -> p q t"))
         nc.scalar.copy(dg_grouped[:, 1], gout_raw[:].rearrange("p t q -> p q t"))
@@ -140,19 +147,26 @@ def tile_attend_hvsoftthreshold_q_kernel(
             "dg", dg_grouped[:].rearrange("p s q t -> p (s q t)"), 2 * Q
         )
         ta_ps = key_scores("ta_ps", "bank_ta", dg_codes[:, 0:Q], dg_scales[:, 0:Q])
-        val_words_g = gather("val_words_g", val_words, U16, "dg_grouped")
+        val_words_g = gather("val_words_g", val_words, U16)
+        val_scales_g = gather("val_scales_g", val_scales, U8)
 
         sig = tile("sig", [P, PACK, P], F32)
         nc.scalar.activation(out=sig[:], in_=dealt(a_ps), func=ACT.Sigmoid, bias=neg_th[:])
         mag = tile("mag", [P, PACK, P], F32)
-        nc.scalar.activation(out=mag[:], in_=dealt(a_ps), func=ACT.Abs, bias=neg_th[:])
-        sig_mag = tile("sig_mag", [P, PACK, P], F32)
-        nc.scalar.activation(out=sig_mag[:], in_=mag[:], func=ACT.Sigmoid)
+        nc.scalar.activation(out=mag[:], in_=sig[:], func=ACT.Abs, bias=-0.5)
         relu = tile("relu", [P, PACK, P], F32)
         relu_sum = column("relu_sum")
         nc.scalar.activation(
             out=relu[:], in_=dealt(a_ps), func=ACT.Relu, bias=neg_th[:], accum_out=relu_sum[:]
         )
+
+        log_sig = tile("log_sig", [P, PACK, P], F32)
+        log_sum = column("log_sum")
+        nc.scalar.activation(out=log_sig[:], in_=mag[:], func=ACT.Ln, bias=0.5, accum_out=log_sum[:])
+        z_part = affine("z_part", relu_sum[:], 1.0, reserve_col[:])
+        z = affine("z", log_sum[:], -1.0, z_part[:])
+        neg_p = tile("neg_p", [P, PACK, P], F32)
+        nc.gpsimd.tensor_tensor(neg_p[:], log_sig[:], relu[:], ALU.subtract)
 
         c0t_ps = ps.tile([P, I // P, Q], F32, name="c0t_ps", tag="bank_c0")
         for j in range(I // P):
@@ -176,15 +190,11 @@ def tile_attend_hvsoftthreshold_q_kernel(
             for j in range(I // P):
                 nc.tensor.transpose(bank[:, j * P : (j + 1) * P], cst[:, j, :], ident[:])
 
-        log_sig = tile("log_sig", [P, PACK, P], F32, "size_col")
-        log_sum = column("log_sum")
-        nc.scalar.activation(out=log_sig[:], in_=sig_mag[:], func=ACT.Ln, accum_out=log_sum[:])
 
-        sums = tile("sums", [P, 3], F32)
-        neg_cs_relu, tz, cs_tp = (sums[:, n : n + 1] for n in range(3))
+        tz = column("tz")
         tp = tile("tp", [P, PACK, P], F32)
         nc.vector.scalar_tensor_tensor(
-            tp[:], dealt(ta_ps), 1.0, sig[:], ALU.mult, ALU.mult, accum_out=tz
+            tp[:], dealt(ta_ps), 1.0, sig[:], ALU.mult, ALU.mult, accum_out=tz[:]
         )
         neg_w = tile("neg_w", [P, PACK, P], F32)
         nc.vector.scalar_tensor_tensor(neg_w[:], sig[:], 1.0, dealt(ta_ps), ALU.subtract, ALU.mult)
@@ -209,22 +219,21 @@ def tile_attend_hvsoftthreshold_q_kernel(
                 product[:], dealt(cs_v), sign, other[:], ALU.mult, ALU.mult, accum_out=total
             )
 
-        def affine(name, x, scale, bias=None, shape=(P, 1)):
-            y = tile(name, list(shape), F32)
-            if bias is None:
-                nc.scalar.activation(out=y[:], in_=x, func=ACT.Copy, scale=scale)
-            else:
-                nc.scalar.activation(out=y[:], in_=x, func=ACT.Identity, scale=scale, bias=bias)
-            return y
-
-        z_part = affine("z_part", relu_sum[:], 1.0, reserve_col[:])
-        two_tz = affine("two_tz", tz, 2.0)
-        kt_first = tile("kt_first", [P, 1, P, PACK], BF16)
-        weave(kt_first[:, 0], turn_key_rows(0))
-        weighted_sum("cs_tp", 1.0, tp, cs_tp, "key_rows0")
-        weighted_sum("cs_relu", -1.0, relu, neg_cs_relu)
-        turned1 = turn_key_rows(1, "relu")
-        z = affine("z", log_sum[:], -1.0, z_part[:])
+        turned0 = turn_key_rows(0)
+        turned1 = turn_key_rows(1)
+        r = column("r", "key_rows1")
+        nc.vector.reciprocal(r[:], z[:])
+        sums = tile("sums", [P, 2], F32)
+        weighted_sum("k_tp", r[:], tp, sums[:, 0:1])
+        weighted_sum("k_p", r[:], neg_p, sums[:, 1:2])
+        tz_r = affine("tz_r", tz[:], r[:])
+        tz_r2 = affine("tz_r2", tz_r[:], r[:])
+        two_tz_r = affine("two_tz_r", tz_r[:], 2.0)
+        scaled = affine("scaled", sums[:], r[:], shape=(P, 2))
+        dz = scaled[:, 1:2]
+        neg_tdz = affine("neg_tdz", dz, two_tz_r[:], scaled[:, 0:1])
+        k = affine("k", dealt(cs_s), r[:], shape=(P, PACK, P))
+        neg_tdp = affine("neg_tdp", dealt(cs_s), tz_r2[:], neg_tdz[:], shape=(P, PACK, P))
 
         sig_t = ps.tile([P, PACK, Q], F32, name="sig_t")
         for t in range(PACK):
@@ -236,27 +245,17 @@ def tile_attend_hvsoftthreshold_q_kernel(
                 out=factor_planes[:, t, :], in_=sig_t[:, t, :], func=ACT.Copy,
                 scale=neg_fs[:, t : t + 1],
             )
-
+        kt_low = tile("kt_low", [P, 2, P, PACK], BF16)
+        weave(kt_low[:, 0], turned0)
+        weave(kt_low[:, 1], turned1)
         factor = tile("factor", [P, Q, PACK], F32)
         nc.scalar.copy(factor[:], factor_planes[:].rearrange("p t q -> p q t"))
-        r = column("r", "key_rows1")
-        nc.vector.reciprocal(r[:], z[:])
-        cs_log = column("cs_log")
-        weighted_sum("cs_log", 1.0, log_sig, cs_log[:])
-        turned2 = turn_key_rows(2, "size_col")
-        r2 = column("r2")
-        nc.scalar.activation(out=r2[:], in_=r[:], func=ACT.Square)
-        scaled = affine("scaled", sums[:], r2[:], shape=(P, 3))
-        dz_factor = affine("dz_factor", two_tz[:], r[:])
-        dz = affine("dz", cs_log[:], r2[:], scaled[:, 0:1])
-        neg_tdz = affine("neg_tdz", dz[:], dz_factor[:], scaled[:, 2:3])
-        k = affine("k", dealt(cs_s), r[:], shape=(P, PACK, P))
-        neg_tdp = affine("neg_tdp", dealt(cs_s), scaled[:, 1:2], neg_tdz[:], shape=(P, PACK, P))
+
+        turned2 = turn_key_rows(2)
         curve = tile("curve", [P, PACK, P], F32, "key_rows2")
-        nc.vector.scalar_tensor_tensor(curve[:], k[:], dz[:], neg_w[:], ALU.add, ALU.mult)
-        kt_mid = tile("kt_mid", [P, 2, P, PACK], BF16, "neg_tdz")
-        weave(kt_mid[:, 0], turned1)
-        weave(kt_mid[:, 1], turned2)
+        nc.vector.scalar_tensor_tensor(curve[:], k[:], dz, neg_w[:], ALU.add, ALU.mult)
+        kt_high = tile("kt_high", [P, 2, P, PACK], BF16)
+        weave(kt_high[:, 0], turned2)
 
         tda_t = ps.tile([P, PACK, Q], F32, name="tda_t", tag="bank_a")
         for n, part in enumerate((neg_tdp, curve)):
@@ -265,21 +264,19 @@ def tile_attend_hvsoftthreshold_q_kernel(
                     tda_t[:, t, :], lhsT=part[:, t, :], rhs=ident[:], is_transpose=True,
                     start=(n == 0 and t == 0), stop=(n == 1 and t == PACK - 1),
                 )
-        kt_last = tile("kt_last", [P, 1, P, PACK], BF16)
-        weave(kt_last[:, 0], turn_key_rows(3, "neg_w"))
-        kt_quant = [quantize_kt("kt0", kt_first, 1), quantize_kt("kt1", kt_mid, 2, "key_rows3")]
-        gs_words = tile("gs_words", [P, Q, PACK], BF16, "neg_tdz")
+        low = quantize_kt("kt_low", kt_low, 2)
+        weave(kt_high[:, 1], turn_key_rows(3))
+        gs_words = tile("gs_words", [P, Q, PACK], BF16, "key_rows3")
         nc.vector.tensor_tensor(
             gs_words[:], tda_t[:].rearrange("p t q -> p q t"), factor[:], ALU.mult
         )
         gs_codes, gs_scales = quantize("gs", gs_words[:].rearrange("p q t -> p (q t)"), Q)
-        kt_quant.append(quantize_kt("kt2", kt_last, 1))
+        high = quantize_kt("kt_high", kt_high, 2)
 
-        for n, (first, last, bank) in enumerate(((0, 1, "bank_ta"), (1, 3, "bank_c0"), (3, 4, "cs_s"))):
-            width = (last - first) * P
-            cols = slice(first * P, last * P)
-            codes, scales = kt_quant[n]
-            gq = ps.tile([P, width], F32, name="gq%d" % n, tag=bank)
+        half = D // 2
+        for h, (codes, scales) in enumerate((low, high)):
+            cols = slice(h * half, (h + 1) * half)
+            gq = ps.tile([P, half], F32, name="gq%d" % h, tag=("bank_ta", "bank_c0")[h])
             nc.tensor.matmul_mx(
                 out=gq[:],
                 lhsT=gs_codes[:].bitcast(FP8X4),
@@ -289,6 +286,6 @@ def tile_attend_hvsoftthreshold_q_kernel(
                 start=True,
                 stop=True,
             )
-            result = tile("result%d" % n, [P, width], F32)
+            result = tile("result%d" % h, [P, half], F32)
             nc.vector.tensor_tensor(result[:], gq[:], res_sb[:, cols], ALU.add)
             nc.sync.dma_start(out[:, cols], result[:])

@@ -179,7 +179,7 @@ def tile_attend_hvsoftthreshold_q_kernel(
                 start=True,
                 stop=True,
             )
-        cst = tile("cst", [P, I // P, Q], F32)
+        cst = tile("cst", [P, I // P, Q], F32, "mag")
         for j in range(I // P):
             nc.scalar.activation(
                 out=cst[:, j, :], in_=c0t_ps[:, j, :], func=ACT.Copy, scale=size_col[:, j : j + 1]
@@ -196,8 +196,10 @@ def tile_attend_hvsoftthreshold_q_kernel(
         nc.vector.scalar_tensor_tensor(
             tp[:], dealt(ta_ps), 1.0, sig[:], ALU.mult, ALU.mult, accum_out=tz[:]
         )
+        ta = tile("ta", [P, PACK, P], F32, "mag")
+        nc.scalar.copy(ta[:], dealt(ta_ps))
         neg_w = tile("neg_w", [P, PACK, P], F32)
-        nc.vector.scalar_tensor_tensor(neg_w[:], sig[:], 1.0, dealt(ta_ps), ALU.subtract, ALU.mult)
+        nc.gpsimd.tensor_tensor(neg_w[:], tp[:], ta[:], ALU.subtract)
 
         def turn_key_rows(c, tag=None):
             picked = gather("kt_picked%d" % c, key_rows[c], BF16, tag)
@@ -221,6 +223,9 @@ def tile_attend_hvsoftthreshold_q_kernel(
 
         turned0 = turn_key_rows(0)
         turned1 = turn_key_rows(1)
+        kt_low = tile("kt_low", [P, 2, P, PACK], BF16)
+        weave(kt_low[:, 0], turned0)
+        weave(kt_low[:, 1], turned1)
         r = column("r", "key_rows1")
         nc.vector.reciprocal(r[:], z[:])
         sums = tile("sums", [P, 2], F32)
@@ -231,8 +236,8 @@ def tile_attend_hvsoftthreshold_q_kernel(
         two_tz_r = affine("two_tz_r", tz_r[:], 2.0)
         scaled = affine("scaled", sums[:], r[:], shape=(P, 2))
         dz = scaled[:, 1:2]
+        dp = affine("dp", dealt(cs_s), r[:], dz, shape=(P, PACK, P))
         neg_tdz = affine("neg_tdz", dz, two_tz_r[:], scaled[:, 0:1])
-        k = affine("k", dealt(cs_s), r[:], shape=(P, PACK, P))
         neg_tdp = affine("neg_tdp", dealt(cs_s), tz_r2[:], neg_tdz[:], shape=(P, PACK, P))
 
         sig_t = ps.tile([P, PACK, Q], F32, name="sig_t")
@@ -245,15 +250,12 @@ def tile_attend_hvsoftthreshold_q_kernel(
                 out=factor_planes[:, t, :], in_=sig_t[:, t, :], func=ACT.Copy,
                 scale=neg_fs[:, t : t + 1],
             )
-        kt_low = tile("kt_low", [P, 2, P, PACK], BF16)
-        weave(kt_low[:, 0], turned0)
-        weave(kt_low[:, 1], turned1)
         factor = tile("factor", [P, Q, PACK], F32)
         nc.scalar.copy(factor[:], factor_planes[:].rearrange("p t q -> p q t"))
 
         turned2 = turn_key_rows(2)
-        curve = tile("curve", [P, PACK, P], F32, "key_rows2")
-        nc.vector.scalar_tensor_tensor(curve[:], k[:], dz, neg_w[:], ALU.add, ALU.mult)
+        curve = tile("curve", [P, PACK, P], F32)
+        nc.gpsimd.tensor_tensor(curve[:], dp[:], neg_w[:], ALU.mult)
         kt_high = tile("kt_high", [P, 2, P, PACK], BF16)
         weave(kt_high[:, 0], turned2)
 
@@ -264,7 +266,7 @@ def tile_attend_hvsoftthreshold_q_kernel(
                     tda_t[:, t, :], lhsT=part[:, t, :], rhs=ident[:], is_transpose=True,
                     start=(n == 0 and t == 0), stop=(n == 1 and t == PACK - 1),
                 )
-        low = quantize_kt("kt_low", kt_low, 2)
+        low = quantize_kt("kt_low", kt_low, 2, "key_rows2")
         weave(kt_high[:, 1], turn_key_rows(3))
         gs_words = tile("gs_words", [P, Q, PACK], BF16, "key_rows3")
         nc.vector.tensor_tensor(

from contextlib import ExitStack

import concourse.mybir as mybir
from concourse.masks import make_identity

F32 = mybir.dt.float32
BF16 = mybir.dt.bfloat16
I32 = mybir.dt.int32
U32 = mybir.dt.uint32
U16 = mybir.dt.uint16
U8 = mybir.dt.uint8
FP8X4 = mybir.dt.float8_e4m3fn_x4
FP4X4 = mybir.dt.float4_e2m1fn_x4
ALU = mybir.AluOpType
ACT = mybir.ActivationFunctionType

P = 128
PACK = 4
D, E, T, I, Q = 512, 512, 2048, 512, 128
FLOPS = 2 * Q * I * (2 * D + E + D)


def tile_attend_hvsoftthreshold_q_kernel(
    tc, query, keys_words, keys_scales, th, reserve, gout, vals_words, vals_scales,
    size, dquery, fs, keyrows, res, offs, out,
):
    nc = tc.nc
    with ExitStack() as ctx:
        sb = ctx.enter_context(tc.tile_pool(name="sb", bufs=1))
        ps = ctx.enter_context(tc.psum_pool(name="ps", bufs=1))

        def tile(name, shape, dtype, tag=None):
            return sb.tile(shape, dtype, name=name, tag=tag or name, align_bytes=64)

        def column(name, tag=None):
            return tile(name, [P, 1], F32, tag)

        def dealt(bank):
            return bank[:].rearrange("q (p t) -> q t p", t=PACK)

        key_scales = tile("key_scales", [P, T], U8)
        val_scales = tile("val_scales", [P, T], U8)
        nc.vector.memset(key_scales[:].bitcast(I32), 0)
        nc.vector.memset(val_scales[:].bitcast(I32), 0)
        warm_in = column("warm_in")
        warm_out = column("warm_out")
        nc.vector.memset(warm_in[:], 0.0)
        nc.scalar.activation(out=warm_out[:], in_=warm_in[:], func=ACT.Sigmoid)

        offsets = sb.tile([P, I // 16], U16, name="offsets")
        nc.sync.dma_start(offsets[:], offs)

        def load_words(name, words):
            pool_words = tile(name, [P, T], U16)
            nc.sync.dma_start(pool_words[:].bitcast(I32), words[0].bitcast(I32))
            return pool_words

        def load_scales(plane, scales):
            for quad in range(4):
                nc.sync.dma_start(
                    plane[32 * quad : 32 * quad + 4, :].bitcast(I32),
                    scales[0, 4 * quad : 4 * quad + 4, :].bitcast(I32),
                )

        def load_rows(name, rows):
            raw = tile(name, [P, PACK, Q], F32)
            nc.sync.dma_start(raw[:], rows.rearrange("(p t) q -> p t q", t=PACK))
            return raw

        load_scales(key_scales, keys_scales)
        key_words = load_words("key_words", keys_words)
        query_raw = load_rows("query_raw", query)
        dquery_raw = load_rows("dquery_raw", dquery)
        gout_raw = load_rows("gout_raw", gout)
        load_scales(val_scales, vals_scales)
        val_words = load_words("val_words", vals_words)
        th_col = column("th_col")
        nc.sync.dma_start(th_col[:], th)
        size_col = tile("size_col", [P, I // P], F32)
        with nc.allow_non_contiguous_dma(reason="one size a partition and slot tile"):
            nc.sync.dma_start(size_col[:], size.rearrange("o (j m) -> m (o j)", m=P))
        key_rows = []

        def load_key_rows(c):
            rows = tile("key_rows%d" % c, [P, T], F32)
            nc.sync.dma_start(rows[:], keyrows[c * P : (c + 1) * P, :])
            key_rows.append(rows)

        load_key_rows(0)
        reserve_col = column("reserve_col")
        nc.sync.dma_start(reserve_col[:], reserve)
        fs_col = tile("fs_col", [P, PACK], F32)
        nc.sync.dma_start(fs_col[:], fs.rearrange("o (p t) -> p (o t)", t=PACK))
        for c in range(1, D // P):
            load_key_rows(c)
        res_sb = tile("res_sb", [P, D], F32)
        nc.sync.dma_start(res_sb[:], res)

        ident = tile("ident", [P, P], F32)
        make_identity(nc, ident[:])
        neg_th = column("neg_th")
        nc.scalar.activation(out=neg_th[:], in_=th_col[:], func=ACT.Copy, scale=-1.0)

        def gather(name, window, dtype, tag=None):
            picked = tile(name, [P, I], dtype, tag)
            nc.vector.tensor_copy(picked[:], window[:].indirect(offsets[:]))
            return picked

        def quantize(name, grouped, columns, tag=None):
            codes = tile(name + "_codes", [P, columns], U32, tag)
            scales = tile(name + "_scales", [P, columns], U8)
            nc.vector.quantize_mx(out=codes[:].bitcast(FP8X4), scales=scales[:], in_=grouped)
            return codes, scales

        def affine(name, x, scale, bias=None, shape=(P, 1)):
            y = tile(name, list(shape), F32)
            if bias is None:
                nc.scalar.activation(out=y[:], in_=x, func=ACT.Copy, scale=scale)
            else:
                nc.scalar.activation(out=y[:], in_=x, func=ACT.Identity, scale=scale, bias=bias)
            return y

        key_words_g = gather("key_words_g", key_words, U16)
        key_scales_g = gather("key_scales_g", key_scales, U8)
        q_grouped = tile("q_grouped", [P, Q, PACK], BF16)
        nc.scalar.copy(q_grouped[:], query_raw[:].rearrange("p t q -> p q t"))
        q_codes, q_scales = quantize("q", q_grouped[:].rearrange("p q t -> p (q t)"), Q)

        def key_scores(name, tag, codes, scales):
            bank = ps.tile([P, I], F32, name=name, tag=tag)
            nc.tensor.matmul_mx(
                out=bank[:],
                lhsT=codes.bitcast(FP8X4),
                lhsT_scale=scales,
                rhs=key_words_g[:].bitcast(FP4X4),
                rhs_scale=key_scales_g[:],
                start=True,
                stop=True,
            )
            return bank

        a_ps = key_scores("a_ps", "bank_a", q_codes[:], q_scales[:])
        dg_grouped = tile("dg_grouped", [P, 2, Q, PACK], BF16)
        nc.scalar.copy(dg_grouped[:, 0], dquery_raw[:].rearrange("p t q -> p q t"))
        nc.scalar.copy(dg_grouped[:, 1], gout_raw[:].rearrange("p t q -> p q t"))
        dg_codes, dg_scales = quantize(
            "dg", dg_grouped[:].rearrange("p s q t -> p (s q t)"), 2 * Q
        )
        ta_ps = key_scores("ta_ps", "bank_ta", dg_codes[:, 0:Q], dg_scales[:, 0:Q])
        val_words_g = gather("val_words_g", val_words, U16)
        val_scales_g = gather("val_scales_g", val_scales, U8)

        sig = tile("sig", [P, PACK, P], F32)
        nc.scalar.activation(out=sig[:], in_=dealt(a_ps), func=ACT.Sigmoid, bias=neg_th[:])
        mag = tile("mag", [P, PACK, P], F32)
        nc.scalar.activation(out=mag[:], in_=sig[:], func=ACT.Abs, bias=-0.5)
        relu = tile("relu", [P, PACK, P], F32)
        relu_sum = column("relu_sum")
        nc.scalar.activation(
            out=relu[:], in_=dealt(a_ps), func=ACT.Relu, bias=neg_th[:], accum_out=relu_sum[:]
        )

        log_sig = tile("log_sig", [P, PACK, P], F32)
        log_sum = column("log_sum")
        nc.scalar.activation(out=log_sig[:], in_=mag[:], func=ACT.Ln, bias=0.5, accum_out=log_sum[:])
        z_part = affine("z_part", relu_sum[:], 1.0, reserve_col[:])
        z = affine("z", log_sum[:], -1.0, z_part[:])
        neg_p = tile("neg_p", [P, PACK, P], F32)
        nc.gpsimd.tensor_tensor(neg_p[:], log_sig[:], relu[:], ALU.subtract)

        c0t_ps = ps.tile([P, I // P, Q], F32, name="c0t_ps", tag="bank_c0")
        for j in range(I // P):
            nc.tensor.matmul_mx(
                out=c0t_ps[:, j, :],
                lhsT=val_words_g[:, j * P : (j + 1) * P].bitcast(FP4X4),
                lhsT_scale=val_scales_g[:, j * P : (j + 1) * P],
                rhs=dg_codes[:, Q : 2 * Q].bitcast(FP8X4),
                rhs_scale=dg_scales[:, Q : 2 * Q],
                start=True,
                stop=True,
            )
        cst = tile("cst", [P, I // P, Q], F32, "mag")
        for j in range(I // P):
            nc.scalar.activation(
                out=cst[:, j, :], in_=c0t_ps[:, j, :], func=ACT.Copy, scale=size_col[:, j : j + 1]
            )
        cs_v = ps.tile([P, I], F32, name="cs_v")
        cs_s = ps.tile([P, I], F32, name="cs_s", tag="cs_s")
        for bank in (cs_v, cs_s):
            for j in range(I // P):
                nc.tensor.transpose(bank[:, j * P : (j + 1) * P], cst[:, j, :], ident[:])


        tz = column("tz")
        tp = tile("tp", [P, PACK, P], F32)
        nc.vector.scalar_tensor_tensor(
            tp[:], dealt(ta_ps), 1.0, sig[:], ALU.mult, ALU.mult, accum_out=tz[:]
        )
        ta = tile("ta", [P, PACK, P], F32, "mag")
        nc.scalar.copy(ta[:], dealt(ta_ps))
        neg_w = tile("neg_w", [P, PACK, P], F32)
        nc.gpsimd.tensor_tensor(neg_w[:], tp[:], ta[:], ALU.subtract)

        def turn_key_rows(c, tag=None):
            picked = gather("kt_picked%d" % c, key_rows[c], BF16, tag)
            pairs = picked[:].bitcast(F32)
            turned = ps.tile([P, 2, P], F32, name="turned%d" % c, tag="bank_kt%d" % (c % 2))
            for u in range(2):
                nc.tensor.transpose(turned[:, u, :], pairs[:, u : I // 2 : 2], ident[:])
            return turned

        def weave(words, turned):
            nc.scalar.copy(words.bitcast(F32), turned[:].rearrange("p u d -> p d u"))

        def quantize_kt(name, words, chunks, tag=None):
            return quantize(name, words[:].rearrange("p c d t -> p (c d t)"), chunks * P, tag)

        def weighted_sum(name, sign, other, total, tag=None):
            product = tile(name + "_product", [P, PACK, P], F32, tag)
            nc.vector.scalar_tensor_tensor(
                product[:], dealt(cs_v), sign, other[:], ALU.mult, ALU.mult, accum_out=total
            )

        turned0 = turn_key_rows(0)
        turned1 = turn_key_rows(1)
        kt_low = tile("kt_low", [P, 2, P, PACK], BF16)
        weave(kt_low[:, 0], turned0)
        weave(kt_low[:, 1], turned1)
        r = column("r", "key_rows1")
        nc.vector.reciprocal(r[:], z[:])
        sums = tile("sums", [P, 2], F32)
        weighted_sum("k_tp", r[:], tp, sums[:, 0:1])
        weighted_sum("k_p", r[:], neg_p, sums[:, 1:2])
        tz_r = affine("tz_r", tz[:], r[:])
        tz_r2 = affine("tz_r2", tz_r[:], r[:])
        two_tz_r = affine("two_tz_r", tz_r[:], 2.0)
        scaled = affine("scaled", sums[:], r[:], shape=(P, 2))
        dz = scaled[:, 1:2]
        dp = affine("dp", dealt(cs_s), r[:], dz, shape=(P, PACK, P))
        neg_tdz = affine("neg_tdz", dz, two_tz_r[:], scaled[:, 0:1])
        neg_tdp = affine("neg_tdp", dealt(cs_s), tz_r2[:], neg_tdz[:], shape=(P, PACK, P))

        sig_t = ps.tile([P, PACK, Q], F32, name="sig_t")
        for t in range(PACK):
            nc.tensor.transpose(sig_t[:, t, :], sig[:, t, :], ident[:])
        neg_fs = affine("neg_fs", fs_col[:], -1.0, shape=(P, PACK))
        factor_planes = tile("factor_planes", [P, PACK, Q], F32)
        for t in range(PACK):
            nc.scalar.activation(
                out=factor_planes[:, t, :], in_=sig_t[:, t, :], func=ACT.Copy,
                scale=neg_fs[:, t : t + 1],
            )
        factor = tile("factor", [P, Q, PACK], F32)
        nc.scalar.copy(factor[:], factor_planes[:].rearrange("p t q -> p q t"))

        turned2 = turn_key_rows(2)
        curve = tile("curve", [P, PACK, P], F32)
        nc.gpsimd.tensor_tensor(curve[:], dp[:], neg_w[:], ALU.mult)
        kt_high = tile("kt_high", [P, 2, P, PACK], BF16)
        weave(kt_high[:, 0], turned2)

        tda_t = ps.tile([P, PACK, Q], F32, name="tda_t", tag="bank_a")
        for n, part in enumerate((neg_tdp, curve)):
            for t in range(PACK):
                nc.tensor.matmul(
                    tda_t[:, t, :], lhsT=part[:, t, :], rhs=ident[:], is_transpose=True,
                    start=(n == 0 and t == 0), stop=(n == 1 and t == PACK - 1),
                )
        low = quantize_kt("kt_low", kt_low, 2, "key_rows2")
        weave(kt_high[:, 1], turn_key_rows(3))
        gs_words = tile("gs_words", [P, Q, PACK], BF16, "key_rows3")
        nc.vector.tensor_tensor(
            gs_words[:], tda_t[:].rearrange("p t q -> p q t"), factor[:], ALU.mult
        )
        gs_codes, gs_scales = quantize("gs", gs_words[:].rearrange("p q t -> p (q t)"), Q)
        high = quantize_kt("kt_high", kt_high, 2)

        half = D // 2
        for h, (codes, scales) in enumerate((low, high)):
            cols = slice(h * half, (h + 1) * half)
            gq = ps.tile([P, half], F32, name="gq%d" % h, tag=("bank_ta", "bank_c0")[h])
            nc.tensor.matmul_mx(
                out=gq[:],
                lhsT=gs_codes[:].bitcast(FP8X4),
                lhsT_scale=gs_scales[:],
                rhs=codes[:].bitcast(FP8X4),
                rhs_scale=scales[:],
                start=True,
                stop=True,
            )
            result = tile("result%d" % h, [P, half], F32)
            nc.vector.tensor_tensor(result[:], gq[:], res_sb[:, cols], ALU.add)
            nc.sync.dma_start(out[:, cols], result[:])
